import numpy as np
import ml_dtypes


def mxq(x, axis, fmt="e4m3"):
    dtype, down = {"e4m3": (ml_dtypes.float8_e4m3fn, 7), "e5m2": (ml_dtypes.float8_e5m2, 14)}[fmt]
    v = np.moveaxis(np.asarray(x, np.float32).astype(ml_dtypes.bfloat16).astype(np.float64), axis, -1)
    blocks = v.reshape(v.shape[:-1] + (-1, 32))
    amax = np.abs(blocks).max(-1, keepdims=True)
    byte = np.maximum(np.where(amax > 0, np.frexp(amax)[1] - 1 + 127, 0) - down, 1)
    scale = np.exp2(byte - 127.0)
    codes = (blocks / scale).astype(np.float32).astype(dtype).astype(np.float64)
    return np.moveaxis((codes * scale).reshape(v.shape), -1, axis)


WIDE = False


def mx_kscale(k, group=512):
    if not WIDE:
        return np.ones(k)
    levels = np.array([10, -10, 5, -5, 0])
    if group != 512:
        return np.exp2(np.random.permutation(np.resize(levels, k // group))).repeat(group)
    if k % 512:
        return np.exp2(np.random.permutation(np.resize(levels, k // 32))).repeat(32)
    a = np.empty((k // 512, 16))
    for p in range(k // 512):
        a[p, :8] = np.random.permutation(np.resize(levels, 8))
        for g in range(8):
            far = levels[np.abs(levels - a[p, g]) >= 10]
            a[p, g + 8] = far[np.random.randint(len(far))]
    return np.exp2(a.ravel()).repeat(32)


def f64(x):
    return np.asarray(x).astype(np.float64)


E2M1 = np.array([0.0, 0.5, 1.0, 1.5, 2.0, 3.0, 4.0, 6.0, -0.0, -0.5, -1.0, -1.5, -2.0, -3.0, -4.0, -6.0])


def pack_group(w):
    k, n = w.shape
    w = f64(np.asarray(w, np.float32).astype(ml_dtypes.bfloat16)).reshape(k // 32, 32, n)
    amax = np.abs(w).max(1)
    mant, ex = np.frexp(amax / 6.0)
    byte = np.clip(np.where(amax > 0, np.where(mant > 0.5, ex, ex - 1) + 127, 1), 1, 254)
    scaled = (w * np.exp2(127.0 - byte)[:, None, :]).reshape(k, n).astype(np.float32)
    c = np.ascontiguousarray(scaled.reshape(k // 4, 4, n).transpose(0, 2, 1)).astype(ml_dtypes.float4_e2m1fn).view(np.uint8) & 0xF
    return np.ascontiguousarray((c[..., 0::2] | (c[..., 1::2] << 4)).reshape(k // 4, 2 * n)), byte.astype(np.uint8)


def unpack_group(words, scales):
    p, n = words.shape[0], scales.shape[1]
    words = np.ascontiguousarray(words).reshape(p, n, 2)
    nib = np.empty((p, n, 4), np.uint8)
    nib[..., 0::2] = words & 0xF
    nib[..., 1::2] = words >> 4
    return E2M1[nib].transpose(0, 2, 1).reshape(4 * p, n) * np.repeat(np.exp2(scales.astype(np.float64) - 127.0), 32, axis=0)


def softplus(v):
    return np.log(1.0 + np.exp(v))


def sigmoid(v):
    return 1.0 / (1.0 + np.exp(-v))


G, D, M, O, N = 2, 256, 256, 256, 512


def setup_inputs():
    n = np.random.standard_normal
    s_d = mx_kscale(D, 0)
    s_o = mx_kscale(O, 0)
    w1_ = [pack_group(w) for w in n((G, D, M)) / np.sqrt(D) / s_d[:, None]]
    w2_ = [pack_group(w) for w in n((G, D, M)) / np.sqrt(D) / s_d[:, None]]
    wo_ = [pack_group(w) for w in n((G, O, M)) / np.sqrt(O) / s_o[:, None]]
    return {
        "x": (n((G, D, N)) * s_d[:, None]).astype(np.float32),
        "w1_words": np.stack([w[0] for w in w1_]),
        "w1_scales": np.stack([w[1] for w in w1_]),
        "w2_words": np.stack([w[0] for w in w2_]),
        "w2_scales": np.stack([w[1] for w in w2_]),
        "re": (np.random.uniform(50.0, 200.0, (G, M, 1))).astype(np.float32),
        "wo_words": np.stack([w[0] for w in wo_]),
        "wo_scales": np.stack([w[1] for w in wo_]),
        "dy": (n((G, O, N)) * s_o[:, None]).astype(np.float32),
        "old": (0.3 * n((G, M, N))).astype(np.float32),
    }


def reference(x, w1_words, w1_scales, w2_words, w2_scales, re, wo_words, wo_scales, dy, old):
    w1 = np.stack([unpack_group(w1_words[g], w1_scales[g]) for g in range(G)])
    xq = mxq(f64(x), 1, "e4m3")
    z1 = w1.transpose(0, 2, 1) @ xq
    w2 = np.stack([unpack_group(w2_words[g], w2_scales[g]) for g in range(G)])
    z2 = w2.transpose(0, 2, 1) @ xq
    p1 = softplus(z1)
    zs = np.sum(p1, axis=-1, keepdims=True) + f64(re)
    wo = np.stack([unpack_group(wo_words[g], wo_scales[g]) for g in range(G)])
    dyq = mxq(f64(dy), 1, "e4m3")
    c0 = wo.transpose(0, 2, 1) @ dyq
    dzs = np.sum(c0 * 512.0 * np.tanh(z2) * p1 / np.square(zs) * (-1.0), axis=-1, keepdims=True)
    dp1 = c0 * 512.0 * np.tanh(z2) / zs + dzs
    dz1 = dp1 * sigmoid(z1)
    y = dz1 + f64(old)
    return y

@@ -1,0 +1,215 @@
+from contextlib import ExitStack
+
+import concourse.mybir as mybir
+
+G, D, M, N = 2, 256, 256, 512
+FLOPS = 3 * 2 * G * D * M * N
+
+F32 = mybir.dt.float32
+BF16 = mybir.dt.bfloat16
+I32 = mybir.dt.int32
+U32 = mybir.dt.uint32
+U8 = mybir.dt.uint8
+FP8X4 = mybir.dt.float8_e4m3fn_x4
+FP4X4 = mybir.dt.float4_e2m1fn_x4
+ALU = mybir.AluOpType
+ACT = mybir.ActivationFunctionType
+
+P = 128
+PACK = 4
+ROWS = D // PACK
+HALF = N // 2
+VECTOR_EXTRA = 64
+BLOCKS = [(g, h) for h in range(M // P) for g in range(G)]
+
+
+def tile_rows_browshare_kernel(tc, x, w1_words, w1_scales, w2_words, w2_scales, re,
+                                   wo_words, wo_scales, dy, old, out):
+    nc = tc.nc
+    nb = len(BLOCKS)
+    with ExitStack() as ctx:
+        sb = ctx.enter_context(tc.tile_pool(name="sb", bufs=1))
+        ps = ctx.enter_context(tc.psum_pool(name="ps", bufs=1))
+        ctx.enter_context(tc.manual_schedule())
+
+        def per_block(name, width):
+            return [sb.tile([P, width], F32, name=name + "%d" % k) for k in range(nb)]
+
+        x_raw = sb.tile([P, PACK, N], F32)
+        dy_raw = sb.tile([P, PACK, N], F32)
+        old_sb = sb.tile([P, G, M // P, N], F32)
+        re_sb = sb.tile([P, G, M // P], F32)
+        w_words = [sb.tile([P, 2 * M], U8, name="w_words%d" % i, align_bytes=64) for i in range(3)]
+        w_scales = sb.tile([P, 3 * M], U8, align_bytes=64)
+        x_bf = [sb.tile([P, HALF * PACK], BF16, name="x_bf%d" % i, align_bytes=64) for i in range(2)]
+        dy_bf = [sb.tile([P, HALF * PACK], BF16, name="dy_bf%d" % i, align_bytes=64) for i in range(2)]
+        x_codes = sb.tile([P, N], U32, align_bytes=64)
+        x_scales = sb.tile([P, N], U8, align_bytes=64)
+        dy_codes = sb.tile([P, N], U32, align_bytes=64)
+        dy_scales = sb.tile([P, N], U8, align_bytes=64)
+        warm_in = sb.tile([P, 1], F32)
+        warm_out = sb.tile([P, 1], F32)
+
+        z1 = [ps.tile([P, N], F32, name="z1_%d" % k) for k in range(nb)]
+        zc = [ps.tile([P, N], F32, name="zc_%d" % k) for k in range(nb)]
+
+        tanh_z2 = per_block("tanh_z2", N)
+        sig = per_block("sig", N)
+        dist = per_block("dist", N)
+        logsig = per_block("logsig", N)
+        relu_z1 = per_block("relu_z1", N)
+        a = per_block("a", N)
+        a_relu = per_block("a_relu", N)
+        a_log = per_block("a_log", N)
+        q = per_block("q", N)
+        y = per_block("y", N)
+        sum_relu = per_block("sum_relu", 1)
+        sum_log = per_block("sum_log", 1)
+        sum_a_relu = per_block("sum_a_relu", 1)
+        sum_a_log = per_block("sum_a_log", 1)
+        zs = per_block("zs", 1)
+        rz = per_block("rz", 1)
+        mean = per_block("mean", 1)
+
+        W1, W2, WO = 0, 1, 2
+
+        def load_rows(dst, src):
+            nc.sync.dma_start(out=dst[:], in_=src.rearrange("g (p j) n -> (g p) j n", j=PACK))
+
+        def load_words(i, src):
+            nc.sync.dma_start(out=w_words[i][:].bitcast(I32),
+                              in_=src.rearrange("g p b -> (g p) b").bitcast(I32))
+
+        def load_scales(queue, i, src):
+            rows = src.rearrange("g t m -> (g t) m")
+            for quad in range(4):
+                queue.dma_start(out=w_scales[32 * quad:32 * quad + 4, M * i:M * (i + 1)].bitcast(I32),
+                                in_=rows[4 * quad:4 * quad + 4, :].bitcast(I32))
+
+        def interleave(copy, dst, raw, half, c0, c1):
+            dst_view = dst[half][:, PACK * c0:PACK * c1].rearrange("p (c i j) -> p c j i", i=4, j=PACK)
+            src_view = raw[:, :, HALF * half + c0:HALF * half + c1].rearrange("p j (c i) -> p c j i", i=4)
+            copy(out=dst_view, in_=src_view)
+
+        def quantize(codes, scales, src, half):
+            cols = slice(HALF * half, HALF * (half + 1))
+            nc.vector.quantize_mx(out=codes[:, cols].bitcast(FP8X4), scales=scales[:, cols], in_=src[half][:])
+
+        def product(bank, i, codes, scales, k):
+            g, h = BLOCKS[k]
+            rows = slice(ROWS * g, ROWS * (g + 1))
+            nc.tensor.matmul_mx(
+                out=bank[k][:],
+                lhsT=w_words[i][rows, 2 * P * h:2 * P * (h + 1)].bitcast(FP4X4),
+                lhsT_scale=w_scales[rows, M * i + P * h:M * i + P * (h + 1)],
+                rhs=codes[rows, :].bitcast(FP8X4),
+                rhs_scale=scales[rows, :],
+                start=True, stop=True)
+
+        nc.vector.memset(w_scales[:].bitcast(I32), 0)
+        nc.vector.memset(warm_in[:], 0.0)
+        nc.scalar.activation(out=warm_out[:], in_=warm_in[:], func=ACT.Sigmoid)
+        load_rows(x_raw, x)
+        load_words(W2, w2_words)
+        load_scales(nc.sync, W2, w2_scales)
+        load_words(W1, w1_words)
+        load_rows(dy_raw, dy)
+        load_scales(nc.gpsimd, WO, wo_scales)
+        load_scales(nc.sync, W1, w1_scales)
+        load_words(WO, wo_words)
+        with nc.allow_non_contiguous_dma(reason="one reserve value to a partition"):
+            nc.sync.dma_start(out=re_sb[:], in_=re.rearrange("g (h p) o -> p g (h o)", p=P))
+        nc.sync.dma_start(out=old_sb[:], in_=old.rearrange("g (h p) n -> p g h n", p=P))
+
+        interleave(nc.scalar.copy, x_bf, x_raw, 1, VECTOR_EXTRA, HALF)
+        interleave(nc.vector.tensor_copy, x_bf, x_raw, 0, 0, HALF)
+        interleave(nc.vector.tensor_copy, x_bf, x_raw, 1, 0, VECTOR_EXTRA)
+        quantize(x_codes, x_scales, x_bf, 0)
+        quantize(x_codes, x_scales, x_bf, 1)
+        for k in range(nb):
+            product(zc, W2, x_codes, x_scales, k)
+        for k in range(nb):
+            product(z1, W1, x_codes, x_scales, k)
+        for k in range(nb):
+            nc.scalar.activation(out=tanh_z2[k][:], in_=zc[k][:], func=ACT.Tanh)
+
+        interleave(nc.vector.tensor_copy, dy_bf, dy_raw, 0, 0, HALF)
+        interleave(nc.vector.tensor_copy, dy_bf, dy_raw, 1, 0, HALF)
+        quantize(dy_codes, dy_scales, dy_bf, 0)
+        quantize(dy_codes, dy_scales, dy_bf, 1)
+        for k in range(nb):
+            product(zc, WO, dy_codes, dy_scales, k)
+
+        nc.vector.tensor_scalar(out=relu_z1[0][:], in0=z1[0][:], scalar1=0.0, scalar2=None,
+                                op0=ALU.max, op1=ALU.add, accum_out=sum_relu[0][:])
+        for k in range(nb):
+            nc.scalar.activation(out=sig[k][:], in_=z1[k][:], func=ACT.Sigmoid)
+
+        def form_a(k):
+            nc.vector.scalar_tensor_tensor(out=a[k][:], in0=zc[k][:], scalar=512.0, in1=tanh_z2[k][:],
+                                           op0=ALU.mult, op1=ALU.mult)
+
+        def form_a_relu(k):
+            nc.vector.scalar_tensor_tensor(out=a_relu[k][:], in0=z1[k][:], scalar=0.0, in1=a[k][:],
+                                           op0=ALU.max, op1=ALU.mult, accum_out=sum_a_relu[k][:])
+
+        def form_dist(k):
+            nc.scalar.activation(out=dist[k][:], in_=sig[k][:], func=ACT.Abs, bias=-0.5)
+
+        def form_relu(k):
+            nc.scalar.activation(out=relu_z1[k][:], in_=z1[k][:], func=ACT.Relu, accum_out=sum_relu[k][:])
+
+        def form_log(k):
+            nc.scalar.activation(out=logsig[k][:], in_=dist[k][:], func=ACT.Ln, bias=0.5,
+                                 accum_out=sum_log[k][:])
+
+        def form_zs(k):
+            g, h = BLOCKS[k]
+            nc.vector.tensor_scalar(out=zs[k][:], in0=sum_relu[k][:], scalar1=sum_log[k][:],
+                                    scalar2=re_sb[:, g, h:h + 1], op0=ALU.subtract, op1=ALU.add)
+
+        def form_a_log(k):
+            nc.vector.scalar_tensor_tensor(out=a_log[k][:], in0=logsig[k][:], scalar=1.0, in1=a[k][:],
+                                           op0=ALU.mult, op1=ALU.mult, accum_out=sum_a_log[k][:])
+
+        def form_rz(k):
+            nc.vector.reciprocal(out=rz[k][:], in_=zs[k][:])
+
+        def form_mean(k):
+            nc.vector.tensor_scalar(out=mean[k][:], in0=sum_a_relu[k][:], scalar1=sum_a_log[k][:],
+                                    scalar2=rz[k][:], op0=ALU.subtract, op1=ALU.mult)
+
+        def form_q(k):
+            nc.vector.scalar_tensor_tensor(out=q[k][:], in0=a[k][:], scalar=mean[k][:], in1=sig[k][:],
+                                           op0=ALU.subtract, op1=ALU.mult)
+
+        def form_y(k):
+            g, h = BLOCKS[k]
+            nc.vector.scalar_tensor_tensor(out=y[k][:], in0=q[k][:], scalar=rz[k][:], in1=old_sb[:, g, h, :],
+                                           op0=ALU.mult, op1=ALU.add)
+            nc.sync.dma_start(out=out[g, P * h:P * (h + 1), :], in_=y[k][:])
+
+        form_a(0)
+        for k in range(1, nb):
+            form_a(k)
+            form_a_relu(k - 1)
+
+        form_dist(0)
+        form_log(0)
+        form_zs(0)
+        form_a_log(0)
+        form_rz(0)
+        form_a_relu(nb - 1)
+        form_mean(0)
+        for k in range(1, nb):
+            form_dist(k)
+            form_relu(k)
+            form_log(k)
+            form_q(k - 1)
+            form_zs(k)
+            form_a_log(k)
+            form_rz(k)
+            form_y(k - 1)
+            form_mean(k)
+        form_q(nb - 1)
+        form_y(nb - 1)

@@ -80,11 +80,10 @@ def tile_rows_browshare_kernel(tc, x, w1_words, w1_scales, w2_words, w2_scales, 
             nc.sync.dma_start(out=w_words[i][:].bitcast(I32),
                               in_=src.rearrange("g p b -> (g p) b").bitcast(I32))
 
-        def load_scales(queue, i, src):
-            rows = src.rearrange("g t m -> (g t) m")
-            for quad in range(4):
-                queue.dma_start(out=w_scales[32 * quad:32 * quad + 4, M * i:M * (i + 1)].bitcast(I32),
-                                in_=rows[4 * quad:4 * quad + 4, :].bitcast(I32))
+        def load_scales(queue, i, src, quad):
+            rows = src.rearrange("g t m -> (g t) m")[4 * quad:4 * quad + 4, :].bitcast(I32)
+            queue.dma_start(out=w_scales[32 * quad:32 * quad + 32, M * i:M * (i + 1)].bitcast(I32),
+                            in_=rows.unsqueeze(0).to_broadcast([8, 4, M // 4]))
 
         def interleave(copy, dst, raw, half, c0, c1):
             dst_view = dst[half][:, PACK * c0:PACK * c1].rearrange("p (c i j) -> p c j i", i=4, j=PACK)
@@ -106,17 +105,21 @@ def tile_rows_browshare_kernel(tc, x, w1_words, w1_scales, w2_words, w2_scales, 
                 rhs_scale=scales[rows, :],
                 start=True, stop=True)
 
-        nc.vector.memset(w_scales[:].bitcast(I32), 0)
         nc.vector.memset(warm_in[:], 0.0)
         nc.scalar.activation(out=warm_out[:], in_=warm_in[:], func=ACT.Sigmoid)
         load_rows(x_raw, x)
+        for quad in range(2):
+            load_scales(nc.gpsimd, WO, wo_scales, quad)
         load_words(W2, w2_words)
-        load_scales(nc.sync, W2, w2_scales)
+        for quad in range(4):
+            load_scales(nc.sync, W2, w2_scales, quad)
         load_words(W1, w1_words)
         load_rows(dy_raw, dy)
-        load_scales(nc.gpsimd, WO, wo_scales)
-        load_scales(nc.sync, W1, w1_scales)
+        for quad in range(4):
+            load_scales(nc.sync, W1, w1_scales, quad)
         load_words(WO, wo_words)
+        for quad in range(2, 4):
+            load_scales(nc.sync, WO, wo_scales, quad)
         with nc.allow_non_contiguous_dma(reason="one reserve value to a partition"):
             nc.sync.dma_start(out=re_sb[:], in_=re.rearrange("g (h p) o -> p g (h o)", p=P))
         nc.sync.dma_start(out=old_sb[:], in_=old.rearrange("g (h p) n -> p g h n", p=P))
@@ -179,15 +182,15 @@ def tile_rows_browshare_kernel(tc, x, w1_words, w1_scales, w2_words, w2_scales, 
             nc.vector.tensor_scalar(out=mean[k][:], in0=sum_a_relu[k][:], scalar1=sum_a_log[k][:],
                                     scalar2=rz[k][:], op0=ALU.subtract, op1=ALU.mult)
 
-        def form_q(k):
-            nc.vector.scalar_tensor_tensor(out=q[k][:], in0=a[k][:], scalar=mean[k][:], in1=sig[k][:],
+        def form_q(k, cols=slice(0, N)):
+            nc.vector.scalar_tensor_tensor(out=q[k][:, cols], in0=a[k][:, cols], scalar=mean[k][:], in1=sig[k][:, cols],
                                            op0=ALU.subtract, op1=ALU.mult)
 
-        def form_y(k):
+        def form_y(k, cols=slice(0, N)):
             g, h = BLOCKS[k]
-            nc.vector.scalar_tensor_tensor(out=y[k][:], in0=q[k][:], scalar=rz[k][:], in1=old_sb[:, g, h, :],
+            nc.vector.scalar_tensor_tensor(out=y[k][:, cols], in0=q[k][:, cols], scalar=rz[k][:], in1=old_sb[:, g, h, cols],
                                            op0=ALU.mult, op1=ALU.add)
-            nc.sync.dma_start(out=out[g, P * h:P * (h + 1), :], in_=y[k][:])
+            nc.sync.dma_start(out=out[g, P * h:P * (h + 1), cols], in_=y[k][:, cols])
 
         form_a(0)
         for k in range(1, nb):
@@ -211,5 +214,8 @@ def tile_rows_browshare_kernel(tc, x, w1_words, w1_scales, w2_words, w2_scales, 
             form_rz(k)
             form_y(k - 1)
             form_mean(k)
-        form_q(nb - 1)
-        form_y(nb - 1)
+        halves = [slice(0, HALF), slice(HALF, N)]
+        for cols in halves:
+            form_q(nb - 1, cols)
+        for cols in halves:
+            form_y(nb - 1, cols)

@@ -20,6 +20,8 @@ PACK = 4
 ROWS = D // PACK
 HALF = N // 2
 VECTOR_EXTRA = 64
+FINISH = [0, 1, 2, 3]
+FIRST = FINISH[0]
 BLOCKS = [(g, h) for h in range(M // P) for g in range(G)]
 
 
@@ -109,16 +111,16 @@ def tile_rows_browshare_kernel(tc, x, w1_words, w1_scales, w2_words, w2_scales, 
         nc.scalar.activation(out=warm_out[:], in_=warm_in[:], func=ACT.Sigmoid)
         load_rows(x_raw, x)
         for quad in range(2):
-            load_scales(nc.gpsimd, WO, wo_scales, quad)
+            load_scales(nc.gpsimd, W1, w1_scales, quad)
         load_words(W2, w2_words)
         for quad in range(4):
             load_scales(nc.sync, W2, w2_scales, quad)
         load_words(W1, w1_words)
         load_rows(dy_raw, dy)
-        for quad in range(4):
+        for quad in range(2, 4):
             load_scales(nc.sync, W1, w1_scales, quad)
         load_words(WO, wo_words)
-        for quad in range(2, 4):
+        for quad in range(4):
             load_scales(nc.sync, WO, wo_scales, quad)
         with nc.allow_non_contiguous_dma(reason="one reserve value to a partition"):
             nc.sync.dma_start(out=re_sb[:], in_=re.rearrange("g (h p) o -> p g (h o)", p=P))
@@ -129,12 +131,21 @@ def tile_rows_browshare_kernel(tc, x, w1_words, w1_scales, w2_words, w2_scales, 
         interleave(nc.vector.tensor_copy, x_bf, x_raw, 1, 0, VECTOR_EXTRA)
         quantize(x_codes, x_scales, x_bf, 0)
         quantize(x_codes, x_scales, x_bf, 1)
-        for k in range(nb):
+        for k in range(nb - 1):
             product(zc, W2, x_codes, x_scales, k)
-        for k in range(nb):
+        product(z1, W1, x_codes, x_scales, 0)
+        product(zc, W2, x_codes, x_scales, nb - 1)
+        for k in range(1, nb):
             product(z1, W1, x_codes, x_scales, k)
-        for k in range(nb):
+        for k in range(nb - 1):
             nc.scalar.activation(out=tanh_z2[k][:], in_=zc[k][:], func=ACT.Tanh)
+        nc.scalar.activation(out=sig[0][:], in_=z1[0][:], func=ACT.Sigmoid)
+        nc.scalar.activation(out=tanh_z2[nb - 1][:], in_=zc[nb - 1][:], func=ACT.Tanh)
+        upper = sb.tile([P, N], F32)
+        half_sig = sb.tile([P, N], F32)
+        nc.gpsimd.tensor_scalar(out=upper[:], in0=sig[0][:], scalar1=1.0, scalar2=0.5, op0=ALU.min, op1=ALU.max)
+        nc.gpsimd.tensor_scalar(out=half_sig[:], in0=sig[0][:], scalar1=0.5, scalar2=0.0, op0=ALU.mult, op1=ALU.add)
+        nc.gpsimd.tensor_tensor(out=dist[0][:], in0=upper[:], in1=half_sig[:], op=ALU.subtract)
 
         interleave(nc.vector.tensor_copy, dy_bf, dy_raw, 0, 0, HALF)
         interleave(nc.vector.tensor_copy, dy_bf, dy_raw, 1, 0, HALF)
@@ -143,9 +154,12 @@ def tile_rows_browshare_kernel(tc, x, w1_words, w1_scales, w2_words, w2_scales, 
         for k in range(nb):
             product(zc, WO, dy_codes, dy_scales, k)
 
-        nc.vector.tensor_scalar(out=relu_z1[0][:], in0=z1[0][:], scalar1=0.0, scalar2=None,
-                                op0=ALU.max, op1=ALU.add, accum_out=sum_relu[0][:])
-        for k in range(nb):
+        def vector_relu(k):
+            nc.vector.tensor_scalar(out=relu_z1[k][:], in0=z1[k][:], scalar1=0.0, scalar2=None,
+                                    op0=ALU.max, op1=ALU.add, accum_out=sum_relu[k][:])
+
+        vector_relu(FINISH[0])
+        for k in range(1, nb):
             nc.scalar.activation(out=sig[k][:], in_=z1[k][:], func=ACT.Sigmoid)
 
         def form_a(k):
@@ -190,6 +204,9 @@ def tile_rows_browshare_kernel(tc, x, w1_words, w1_scales, w2_words, w2_scales, 
             g, h = BLOCKS[k]
             nc.vector.scalar_tensor_tensor(out=y[k][:, cols], in0=q[k][:, cols], scalar=rz[k][:], in1=old_sb[:, g, h, cols],
                                            op0=ALU.mult, op1=ALU.add)
+
+        def store(k, cols=slice(0, N)):
+            g, h = BLOCKS[k]
             nc.sync.dma_start(out=out[g, P * h:P * (h + 1), cols], in_=y[k][:, cols])
 
         form_a(0)
@@ -197,25 +214,28 @@ def tile_rows_browshare_kernel(tc, x, w1_words, w1_scales, w2_words, w2_scales, 
             form_a(k)
             form_a_relu(k - 1)
 
-        form_dist(0)
-        form_log(0)
-        form_zs(0)
-        form_a_log(0)
-        form_rz(0)
-        form_a_relu(nb - 1)
-        form_mean(0)
-        for k in range(1, nb):
+        halves = [slice(0, HALF), slice(HALF, N)]
+        last = FINISH[-1]
+        nc.scalar.activation(out=logsig[0][:], in_=dist[0][:], func=ACT.Ln, scale=2.0, accum_out=sum_log[0][:])
+        form_zs(FIRST)
+        form_a_log(FIRST)
+        form_rz(FIRST)
+        form_a_relu(last)
+        form_mean(FIRST)
+        for prev, k in zip(FINISH, FINISH[1:]):
             form_dist(k)
             form_relu(k)
             form_log(k)
-            form_q(k - 1)
+            form_q(prev)
             form_zs(k)
             form_a_log(k)
             form_rz(k)
-            form_y(k - 1)
+            form_y(prev, halves[0])
             form_mean(k)
-        halves = [slice(0, HALF), slice(HALF, N)]
+            form_y(prev, halves[1])
+            store(prev)
         for cols in halves:
-            form_q(nb - 1, cols)
+            form_q(last, cols)
         for cols in halves:
-            form_y(nb - 1, cols)
+            form_y(last, cols)
+            store(last, cols)

from contextlib import ExitStack

import concourse.mybir as mybir

G, D, M, N = 2, 256, 256, 512
FLOPS = 3 * 2 * G * D * M * N

F32 = mybir.dt.float32
BF16 = mybir.dt.bfloat16
I32 = mybir.dt.int32
U32 = mybir.dt.uint32
U8 = mybir.dt.uint8
FP8X4 = mybir.dt.float8_e4m3fn_x4
FP4X4 = mybir.dt.float4_e2m1fn_x4
ALU = mybir.AluOpType
ACT = mybir.ActivationFunctionType

P = 128
PACK = 4
ROWS = D // PACK
HALF = N // 2
VECTOR_EXTRA = 64
FINISH = [0, 1, 2, 3]
FIRST = FINISH[0]
BLOCKS = [(g, h) for h in range(M // P) for g in range(G)]


def tile_rows_browshare_kernel(tc, x, w1_words, w1_scales, w2_words, w2_scales, re,
                                   wo_words, wo_scales, dy, old, out):
    nc = tc.nc
    nb = len(BLOCKS)
    with ExitStack() as ctx:
        sb = ctx.enter_context(tc.tile_pool(name="sb", bufs=1))
        ps = ctx.enter_context(tc.psum_pool(name="ps", bufs=1))
        ctx.enter_context(tc.manual_schedule())

        def per_block(name, width):
            return [sb.tile([P, width], F32, name=name + "%d" % k) for k in range(nb)]

        x_raw = sb.tile([P, PACK, N], F32)
        dy_raw = sb.tile([P, PACK, N], F32)
        old_sb = sb.tile([P, G, M // P, N], F32)
        re_sb = sb.tile([P, G, M // P], F32)
        w_words = [sb.tile([P, 2 * M], U8, name="w_words%d" % i, align_bytes=64) for i in range(3)]
        w_scales = sb.tile([P, 3 * M], U8, align_bytes=64)
        x_bf = [sb.tile([P, HALF * PACK], BF16, name="x_bf%d" % i, align_bytes=64) for i in range(2)]
        dy_bf = [sb.tile([P, HALF * PACK], BF16, name="dy_bf%d" % i, align_bytes=64) for i in range(2)]
        x_codes = sb.tile([P, N], U32, align_bytes=64)
        x_scales = sb.tile([P, N], U8, align_bytes=64)
        dy_codes = sb.tile([P, N], U32, align_bytes=64)
        dy_scales = sb.tile([P, N], U8, align_bytes=64)
        warm_in = sb.tile([P, 1], F32)
        warm_out = sb.tile([P, 1], F32)

        z1 = [ps.tile([P, N], F32, name="z1_%d" % k) for k in range(nb)]
        zc = [ps.tile([P, N], F32, name="zc_%d" % k) for k in range(nb)]

        tanh_z2 = per_block("tanh_z2", N)
        sig = per_block("sig", N)
        dist = per_block("dist", N)
        logsig = per_block("logsig", N)
        relu_z1 = per_block("relu_z1", N)
        a = per_block("a", N)
        a_relu = per_block("a_relu", N)
        a_log = per_block("a_log", N)
        q = per_block("q", N)
        y = per_block("y", N)
        sum_relu = per_block("sum_relu", 1)
        sum_log = per_block("sum_log", 1)
        sum_a_relu = per_block("sum_a_relu", 1)
        sum_a_log = per_block("sum_a_log", 1)
        zs = per_block("zs", 1)
        rz = per_block("rz", 1)
        mean = per_block("mean", 1)

        W1, W2, WO = 0, 1, 2

        def load_rows(dst, src):
            nc.sync.dma_start(out=dst[:], in_=src.rearrange("g (p j) n -> (g p) j n", j=PACK))

        def load_words(i, src):
            nc.sync.dma_start(out=w_words[i][:].bitcast(I32),
                              in_=src.rearrange("g p b -> (g p) b").bitcast(I32))

        def load_scales(queue, i, src, quad):
            rows = src.rearrange("g t m -> (g t) m")[4 * quad:4 * quad + 4, :].bitcast(I32)
            queue.dma_start(out=w_scales[32 * quad:32 * quad + 32, M * i:M * (i + 1)].bitcast(I32),
                            in_=rows.unsqueeze(0).to_broadcast([8, 4, M // 4]))

        def interleave(copy, dst, raw, half, c0, c1):
            dst_view = dst[half][:, PACK * c0:PACK * c1].rearrange("p (c i j) -> p c j i", i=4, j=PACK)
            src_view = raw[:, :, HALF * half + c0:HALF * half + c1].rearrange("p j (c i) -> p c j i", i=4)
            copy(out=dst_view, in_=src_view)

        def quantize(codes, scales, src, half):
            cols = slice(HALF * half, HALF * (half + 1))
            nc.vector.quantize_mx(out=codes[:, cols].bitcast(FP8X4), scales=scales[:, cols], in_=src[half][:])

        def product(bank, i, codes, scales, k):
            g, h = BLOCKS[k]
            rows = slice(ROWS * g, ROWS * (g + 1))
            nc.tensor.matmul_mx(
                out=bank[k][:],
                lhsT=w_words[i][rows, 2 * P * h:2 * P * (h + 1)].bitcast(FP4X4),
                lhsT_scale=w_scales[rows, M * i + P * h:M * i + P * (h + 1)],
                rhs=codes[rows, :].bitcast(FP8X4),
                rhs_scale=scales[rows, :],
                start=True, stop=True)

        nc.vector.memset(warm_in[:], 0.0)
        nc.scalar.activation(out=warm_out[:], in_=warm_in[:], func=ACT.Sigmoid)
        load_rows(x_raw, x)
        for quad in range(2):
            load_scales(nc.gpsimd, W1, w1_scales, quad)
        load_words(W2, w2_words)
        for quad in range(4):
            load_scales(nc.sync, W2, w2_scales, quad)
        load_words(W1, w1_words)
        load_rows(dy_raw, dy)
        for quad in range(2, 4):
            load_scales(nc.sync, W1, w1_scales, quad)
        load_words(WO, wo_words)
        for quad in range(4):
            load_scales(nc.sync, WO, wo_scales, quad)
        with nc.allow_non_contiguous_dma(reason="one reserve value to a partition"):
            nc.sync.dma_start(out=re_sb[:], in_=re.rearrange("g (h p) o -> p g (h o)", p=P))
        nc.sync.dma_start(out=old_sb[:], in_=old.rearrange("g (h p) n -> p g h n", p=P))

        interleave(nc.scalar.copy, x_bf, x_raw, 1, VECTOR_EXTRA, HALF)
        interleave(nc.vector.tensor_copy, x_bf, x_raw, 0, 0, HALF)
        interleave(nc.vector.tensor_copy, x_bf, x_raw, 1, 0, VECTOR_EXTRA)
        quantize(x_codes, x_scales, x_bf, 0)
        quantize(x_codes, x_scales, x_bf, 1)
        for k in range(nb - 1):
            product(zc, W2, x_codes, x_scales, k)
        product(z1, W1, x_codes, x_scales, 0)
        product(zc, W2, x_codes, x_scales, nb - 1)
        for k in range(1, nb):
            product(z1, W1, x_codes, x_scales, k)
        for k in range(nb - 1):
            nc.scalar.activation(out=tanh_z2[k][:], in_=zc[k][:], func=ACT.Tanh)
        nc.scalar.activation(out=sig[0][:], in_=z1[0][:], func=ACT.Sigmoid)
        nc.scalar.activation(out=tanh_z2[nb - 1][:], in_=zc[nb - 1][:], func=ACT.Tanh)
        upper = sb.tile([P, N], F32)
        half_sig = sb.tile([P, N], F32)
        nc.gpsimd.tensor_scalar(out=upper[:], in0=sig[0][:], scalar1=1.0, scalar2=0.5, op0=ALU.min, op1=ALU.max)
        nc.gpsimd.tensor_scalar(out=half_sig[:], in0=sig[0][:], scalar1=0.5, scalar2=0.0, op0=ALU.mult, op1=ALU.add)
        nc.gpsimd.tensor_tensor(out=dist[0][:], in0=upper[:], in1=half_sig[:], op=ALU.subtract)

        interleave(nc.vector.tensor_copy, dy_bf, dy_raw, 0, 0, HALF)
        interleave(nc.vector.tensor_copy, dy_bf, dy_raw, 1, 0, HALF)
        quantize(dy_codes, dy_scales, dy_bf, 0)
        quantize(dy_codes, dy_scales, dy_bf, 1)
        for k in range(nb):
            product(zc, WO, dy_codes, dy_scales, k)

        def vector_relu(k):
            nc.vector.tensor_scalar(out=relu_z1[k][:], in0=z1[k][:], scalar1=0.0, scalar2=None,
                                    op0=ALU.max, op1=ALU.add, accum_out=sum_relu[k][:])

        vector_relu(FINISH[0])
        for k in range(1, nb):
            nc.scalar.activation(out=sig[k][:], in_=z1[k][:], func=ACT.Sigmoid)

        def form_a(k):
            nc.vector.scalar_tensor_tensor(out=a[k][:], in0=zc[k][:], scalar=512.0, in1=tanh_z2[k][:],
                                           op0=ALU.mult, op1=ALU.mult)

        def form_a_relu(k):
            nc.vector.scalar_tensor_tensor(out=a_relu[k][:], in0=z1[k][:], scalar=0.0, in1=a[k][:],
                                           op0=ALU.max, op1=ALU.mult, accum_out=sum_a_relu[k][:])

        def form_dist(k):
            nc.scalar.activation(out=dist[k][:], in_=sig[k][:], func=ACT.Abs, bias=-0.5)

        def form_relu(k):
            nc.scalar.activation(out=relu_z1[k][:], in_=z1[k][:], func=ACT.Relu, accum_out=sum_relu[k][:])

        def form_log(k):
            nc.scalar.activation(out=logsig[k][:], in_=dist[k][:], func=ACT.Ln, bias=0.5,
                                 accum_out=sum_log[k][:])

        def form_zs(k):
            g, h = BLOCKS[k]
            nc.vector.tensor_scalar(out=zs[k][:], in0=sum_relu[k][:], scalar1=sum_log[k][:],
                                    scalar2=re_sb[:, g, h:h + 1], op0=ALU.subtract, op1=ALU.add)

        def form_a_log(k):
            nc.vector.scalar_tensor_tensor(out=a_log[k][:], in0=logsig[k][:], scalar=1.0, in1=a[k][:],
                                           op0=ALU.mult, op1=ALU.mult, accum_out=sum_a_log[k][:])

        def form_rz(k):
            nc.vector.reciprocal(out=rz[k][:], in_=zs[k][:])

        def form_mean(k):
            nc.vector.tensor_scalar(out=mean[k][:], in0=sum_a_relu[k][:], scalar1=sum_a_log[k][:],
                                    scalar2=rz[k][:], op0=ALU.subtract, op1=ALU.mult)

        def form_q(k, cols=slice(0, N)):
            nc.vector.scalar_tensor_tensor(out=q[k][:, cols], in0=a[k][:, cols], scalar=mean[k][:], in1=sig[k][:, cols],
                                           op0=ALU.subtract, op1=ALU.mult)

        def form_y(k, cols=slice(0, N)):
            g, h = BLOCKS[k]
            nc.vector.scalar_tensor_tensor(out=y[k][:, cols], in0=q[k][:, cols], scalar=rz[k][:], in1=old_sb[:, g, h, cols],
                                           op0=ALU.mult, op1=ALU.add)

        def store(k, cols=slice(0, N)):
            g, h = BLOCKS[k]
            nc.sync.dma_start(out=out[g, P * h:P * (h + 1), cols], in_=y[k][:, cols])

        form_a(0)
        for k in range(1, nb):
            form_a(k)
            form_a_relu(k - 1)

        halves = [slice(0, HALF), slice(HALF, N)]
        last = FINISH[-1]
        nc.scalar.activation(out=logsig[0][:], in_=dist[0][:], func=ACT.Ln, scale=2.0, accum_out=sum_log[0][:])
        form_zs(FIRST)
        form_a_log(FIRST)
        form_rz(FIRST)
        form_a_relu(last)
        form_mean(FIRST)
        for prev, k in zip(FINISH, FINISH[1:]):
            form_dist(k)
            form_relu(k)
            form_log(k)
            form_q(prev)
            form_zs(k)
            form_a_log(k)
            form_rz(k)
            form_y(prev, halves[0])
            form_mean(k)
            form_y(prev, halves[1])
            store(prev)
        for cols in halves:
            form_q(last, cols)
        for cols in halves:
            form_y(last, cols)
            store(last, cols)
